import numpy as np, ml_dtypes
CORES = [16,32,48,64,80]
N = 5
import mx_ref
NC, G = 160, 4
C, C2 = np.float32(0.047), np.float32(0.02102)
BF = ml_dtypes.bfloat16
def cut(t, i, w=512):
    return t[:, w * i:w * i + w]
def tile(rs):
    return np.stack(rs, axis=2).reshape(128, -1).astype(BF)
def layer(w, X):
    out = []
    for i in range(G):
        for t in range(len(X)):
            p = mx_ref.matmul(mx_ref.quantize(cut(w, len(X) * i + t)), X[t])
            z = p if t == 0 else z + p
        out.append(z)
    return out
def act(Z):
    return [np.maximum(z, 0) * C for z in Z]
def act2(Z):
    return [np.maximum(z, 0) * C2 for z in Z]
def setup_inputs(rng):
    def f(*shape):
        return mx_ref.flush((rng.standard_normal(shape, dtype=np.float32) * np.exp2(rng.integers(-2, 3, shape[:-1] + (1,)))).astype(BF))
    return {"x": f(N, 128, 4 * NC), "w1": f(N, 128, G * 512), "w2": f(N, 128, G * 512), "w3": f(N, 128, G * 512)}
def setup_inputs_blocks(rng):
    d = setup_inputs(rng)
    for k in ("x", "w1", "w2", "w3"): d[k] = mx_ref.spread(d[k], rng, 2)
    return d
def setup_inputs_wide(rng):
    d = setup_inputs(rng)
    for k in ("x", "w1", "w2", "w3"): d[k] = mx_ref.flush((d[k].astype(np.float32) * np.exp2(rng.integers(-4, 5, (N, 1, 1))).astype(np.float32)).astype(BF))
    return d
def reference(x, w1, w2, w3, own=None):
    X = [mx_ref.quantize(x[j]) for j in range(N)]
    t = np.stack([np.stack([tile(act(layer(w1[r], [X[c]]))) for c in range(N)]) for r in range(N)])
    uset = t if own is None else own["t"]
    h = np.zeros((N, 128, 4 * NC), BF)
    for c in range(N):
        for r in range(N):
            P = layer(w2[r], [mx_ref.quantize(uset[r][c])])
            Z = P if r == 0 else [z + p for z, p in zip(Z, P)]
        h[c] = tile(act2(Z))
    use = h if own is None else own["h"]
    H = [mx_ref.quantize(use[j]) for j in range(N)]
    y = np.zeros((N, 128, N * G * NC), np.float32)
    for r in range(N):
        for j in range(N):
            Z = layer(w3[r], [H[j]])
            for i in range(G):
                y[r][:, NC * (G * j + i):NC * (G * j + i) + NC] = Z[i]
    return {"t": t, "h": h, "y": y}

@@ -1,0 +1,295 @@
+import numpy as np
+from concourse.bass import DstId, RemoteDMATransfer
+from concourse.mybir import dt, AluOpType, ActivationFunctionType
+
+N = 5
+NC = 160
+G = 4
+TW = G * NC
+SIM_CORES = 96
+C1 = float(np.float32(0.047))
+C2 = float(np.float32(0.02102))
+W_ROAD = (1, 2)
+P_RELAY = 3
+P_DIRECT = 4
+
+FP8 = "float8_e4m3fn_x4"
+SCRATCH = {
+    "xb": ("sbuf", [128, TW], "bfloat16"),
+    "w1b": ("sbuf", [128, G * 512], "bfloat16"),
+    "w2b": ("sbuf", [128, G * 512], "bfloat16"),
+    "w3b": ("sbuf", [128, G * 512], "bfloat16"),
+    "w1q": ("sbuf", [128, 512], FP8), "w1s": ("sbuf", [128, 512], "uint8"),
+    "w2q": ("sbuf", [128, 512], FP8), "w2s": ("sbuf", [128, 512], "uint8"),
+    "w3q": ("sbuf", [128, 512], FP8), "w3s": ("sbuf", [128, 512], "uint8"),
+    "xq": ("sbuf", [128, N * NC], FP8), "xs": ("sbuf", [128, N * NC], "uint8"),
+    "tb": ("sbuf", [128, N * TW], "bfloat16"),
+    "tq": ("sbuf", [128, N * NC], FP8), "ts": ("sbuf", [128, N * NC], "uint8"),
+    "fw1q": ("sbuf", [128, 512], FP8), "fw1s": ("sbuf", [128, 512], "uint8"),
+    "fw2q": ("sbuf", [128, 512], FP8), "fw2s": ("sbuf", [128, 512], "uint8"),
+    "ft1q": ("sbuf", [128, NC], FP8), "ft1s": ("sbuf", [128, NC], "uint8"),
+    "ft2q": ("sbuf", [128, NC], FP8), "ft2s": ("sbuf", [128, NC], "uint8"),
+    "po1": ("sbuf", [128, TW], "float32"), "po2": ("sbuf", [128, TW], "float32"),
+    "pa": ("sbuf", [128, TW], "float32"), "pb": ("sbuf", [128, TW], "float32"),
+    "u": ("sbuf", [128, TW], "float32"), "v": ("sbuf", [128, TW], "float32"),
+    "hb": ("sbuf", [128, TW], "bfloat16"),
+    "hq": ("sbuf", [128, N * NC], FP8), "hs": ("sbuf", [128, N * NC], "uint8"),
+    "yb": ("sbuf", [128, N * TW], "float32"),
+    "rwq": ("sbuf", [128, 256], FP8), "rws": ("sbuf", [128, 256], "uint8"),
+    "rp": ("sbuf", [128, TW // 2], "float32"),
+    "ps": ("psum", [128, 4096], "float32"),
+}
+SEMAPHORES = (["lx", "lw1", "lw2", "lw3", "qx", "qw1", "qw2", "qw3", "qh", "ha", "st", "st2",
+               "sx", "sw", "sp1", "stq", "sp2", "sh", "rwc", "rwp", "rpa", "s1", "s2",
+               "fw1", "fw2", "ft1", "ft2", "pa0", "pa1", "pb"]
+              + ["pe%d" % b for b in range(8)] + ["ev%d" % b for b in range(8)]
+              + ["qt%d" % c for c in range(N)] + ["x%d" % c for c in range(N)] + ["h%d" % c for c in range(N)]
+              + ["u%d" % i for i in range(G)])
+
+
+def bits(m):
+    return [1 << b for b in range(m.bit_length()) if (m >> b) & 1]
+
+
+def groups(m, n):
+    e = bits(m)
+    k = len(e) // n
+    return [sum(e[i * k:(i + 1) * k]) for i in range(n)]
+
+
+def count(m):
+    return len(bits(m))
+
+
+def to(topo, dst, mask, sem, dst_ap, src_ap):
+    rid, pid, _ = topo.addr(dst)
+    return RemoteDMATransfer(dst_ids=[DstId(rid=rid, pnc=pid)], dma_engine_mask=mask, remote_sem=sem, src=src_ap, dst=dst_ap)
+
+
+def by(v):
+    return v.bitcast(dt.uint8)
+
+
+def helpers_of(topo, core):
+    return [k for k in range(SIM_CORES) if topo.chip(k) == topo.chip(core) and topo.die(k) != topo.die(core)][:2]
+
+
+def helper_program(g, core, T, topo, r, half):
+    S = T.sem
+    dests = [T.cores[(r + d) % N] for d in W_ROAD]
+    off = topo.mask(core, dests[0])
+    gm = groups(off, 2)
+    n_in = count(groups(upper(topo, T.cores[r], core, dests[0]), 2)[0])
+    a, b = 256 * half, 256 * half + 256
+    g.wait_ge(S.rwc, n_in)
+    g.remote_dma_fused([to(topo, dests[k], gm[k], S["fw%d" % W_ROAD[k]], by(T["fw%dq" % W_ROAD[k]][:, a:b]), by(T.rwq[:, 0:256]))
+                        for k in range(2)], local_sem=S.s1)
+    g.wait_ge(S.rwp, n_in)
+    g.remote_dma_fused([to(topo, dests[k], gm[k], S["fw%d" % W_ROAD[k]], T["fw%ds" % W_ROAD[k]][:, a:b], T.rws[:, 0:256])
+                        for k in range(2)], local_sem=S.s1)
+    g.wait_ge(S.rpa, n_in)
+    dst = T.cores[(r + P_RELAY) % N]
+    rid, pid, _ = topo.addr(dst)
+    w = TW // 2
+    g.remote_dma(T.pa[:, w * half:w * half + w], T.rp[:, 0:w], S["pa%d" % half], S.s2, pid, rid, topo.mask(core, dst))
+    g.wait_ge(S.s1, 2 * count(off))
+    g.wait_ge(S.s2, count(topo.mask(core, dst)))
+
+
+def upper(topo, core, near, far):
+    return topo.mask(core, near) & ~topo.mask(core, far)
+
+
+def rank_program(g, core, T, topo):
+    S = T.sem
+    r = T.rank_of(core)
+    if r is None:
+        for k, c in enumerate(T.cores):
+            hs = helpers_of(topo, c)
+            if core in hs:
+                helper_program(g, core, T, topo, k, hs.index(core))
+        return
+    helpers = helpers_of(topo, core)
+    others = [(r + d) % N for d in (1, 2, 3, 4)]
+    off = topo.mask(core, T.cores[others[0]])
+    near = upper(topo, core, helpers[0], T.cores[others[0]])
+    off4, off2, near2 = groups(off, 4), groups(off, 2), groups(near, 2)
+    n4, n2, noff = count(off4[0]), count(off2[0]), count(off)
+    te, ve, ac, sy = g.tensor, g.vector, g.scalar, g.sync
+    RELU, COPY = ActivationFunctionType.Relu, ActivationFunctionType.Copy
+    A, B = 0, 4
+    nm, ne = [0] * 8, [0] * 8
+
+    def bank(k):
+        return T.ps[:, 512 * k:512 * k + NC]
+
+    def mm_tile(base, wq, ws, xq, xs, start=True, stop=True):
+        for b in range(G):
+            k = base + b
+            if start and ne[k]:
+                te.wait_ge(S["ev%d" % k], ne[k])
+            ins = te.matmul_mx(bank(k), wq[:, 128 * b:128 * b + 128], ws[:, 128 * b:128 * b + 128], xq, xs, start, stop)
+            if stop:
+                ins.then_inc(S["pe%d" % k], 1)
+                nm[k] += 1
+
+    def evac(base, out, relu):
+        for b in range(G):
+            k = base + b
+            if b % 2 == 0:
+                ac.wait_ge(S["pe%d" % k], nm[k])
+                ins = ac.activation(out(b), bank(k), RELU, scale=C1) if relu else ac.activation(out(b), bank(k), COPY)
+            else:
+                ve.wait_ge(S["pe%d" % k], nm[k])
+                ins = ve.tensor_scalar(out(b), bank(k), 0.0, C1, AluOpType.max, AluOpType.mult) if relu else ve.tensor_copy(out(b), bank(k))
+            ins.then_inc(S["ev%d" % k], 1)
+            ne[k] += 1
+
+    def wait_ev(q, base):
+        m = [(S["ev%d" % k], ne[k]) for k in range(base, base + G)]
+        for s, n in m:
+            q.wait_ge(s, n)
+
+    def xcol(buf, c):
+        return buf[:, NC * c:NC * c + NC]
+
+    def first(base, c):
+        if c != r:
+            te.wait_ge(S["x%d" % c], 2 * n4)
+        mm_tile(base, T.w1q, T.w1s, xcol(T.xq, c), xcol(T.xs, c))
+
+    def act_t(base, c):
+        evac(base, lambda b: T.tb[:, TW * c + b:TW * c + TW:G], True)
+        wait_ev(ve, base)
+        ve.quantize_mx(xcol(T.tq, c), xcol(T.ts, c), T.tb[:, TW * c:TW * c + TW]).then_inc(S["qt%d" % c], 1)
+
+    def second(base, c):
+        te.wait_ge(S["qt%d" % c], 1)
+        mm_tile(base, T.w2q, T.w2s, xcol(T.tq, c), xcol(T.ts, c))
+
+    def copy_p(base, buf):
+        evac(base, lambda b: buf[:, NC * b:NC * b + NC], False)
+
+    def gather(q, s, sem, local):
+        g.remote_dma_fused([to(topo, T.cores[c], off4[k], S["%s%d" % (sem, r)], by(xcol(q, r)), by(xcol(q, r)))
+                            for k, c in enumerate(others)], local_sem=local)
+        g.remote_dma_fused([to(topo, T.cores[c], off4[k], S["%s%d" % (sem, r)], xcol(s, r), xcol(s, r))
+                            for k, c in enumerate(others)], local_sem=local)
+
+    sy.dma_start(T.xb[:], T.x[:]).then_inc(S.lx, 16)
+    sy.dma_start(T.w2b[:], T.w2[:]).then_inc(S.lw2, 16)
+    sy.dma_start(T.w1b[:], T.w1[:]).then_inc(S.lw1, 16)
+    ve.wait_ge(S.lx, 16)
+    ve.quantize_mx(xcol(T.xq, r), xcol(T.xs, r), T.xb[:]).then_inc(S.qx, 1)
+    ve.wait_ge(S.lw2, 16)
+    ve.quantize_mx(T.w2q[:], T.w2s[:], T.w2b[:]).then_inc(S.qw2, 1)
+    ve.wait_ge(S.lw1, 16)
+    ve.quantize_mx(T.w1q[:], T.w1s[:], T.w1b[:]).then_inc(S.qw1, 1)
+
+    g.wait_ge(S.qx, 1)
+    gather(T.xq, T.xs, "x", S.sx)
+    g.wait_ge(S.qw2, 1)
+    g.remote_dma_fused([to(topo, helpers[k], near2[k], S.rwc, by(T.rwq[:, 0:256]), by(T.w2q[:, 256 * k:256 * k + 256])) for k in range(2)],
+                       local_sem=S.sw)
+    g.remote_dma_fused([to(topo, helpers[k], near2[k], S.rwp, T.rws[:, 0:256], T.w2s[:, 256 * k:256 * k + 256]) for k in range(2)],
+                       local_sem=S.sw)
+    sy.wait_ge(S.sx, 2 * noff)
+    sy.dma_start(T.w3b[:], T.w3[:]).then_inc(S.lw3, 16)
+
+    q1, q2, p1, p2 = [(r + d) % N for d in (W_ROAD[0], W_ROAD[1], P_RELAY, P_DIRECT)]
+    te.wait_ge(S.qx, 1)
+    te.wait_ge(S.qw1, 1)
+    first(A, r)
+    act_t(A, r)
+    first(B, p1)
+    act_t(B, p1)
+    first(A, q1)
+    act_t(A, q1)
+    te.wait_ge(S.qw2, 1)
+    second(B, p1)
+    copy_p(B, T.po1)
+    wait_ev(g, B)
+    g.remote_dma_fused([to(topo, helpers[k], near2[k], S.rpa, T.rp[:, 0:TW // 2], T.po1[:, TW // 2 * k:TW // 2 * k + TW // 2])
+                        for k in range(2)], local_sem=S.sp1)
+    first(A, q2)
+    act_t(A, q2)
+    g.wait_ge(S["qt%d" % q1], 1)
+    g.wait_ge(S["qt%d" % q2], 1)
+    g.remote_dma_fused([to(topo, T.cores[c], off2[k], S["ft%d" % W_ROAD[k]], by(T["ft%dq" % W_ROAD[k]][:, 0:NC]), by(xcol(T.tq, c)))
+                        for k, c in enumerate((q1, q2))], local_sem=S.stq)
+    g.remote_dma_fused([to(topo, T.cores[c], off2[k], S["ft%d" % W_ROAD[k]], T["ft%ds" % W_ROAD[k]][:, 0:NC], xcol(T.ts, c))
+                        for k, c in enumerate((q1, q2))], local_sem=S.stq)
+    first(B, p2)
+    act_t(B, p2)
+    second(A, p2)
+    copy_p(A, T.po2)
+    wait_ev(g, A)
+    rid, pid, _ = topo.addr(T.cores[p2])
+    g.remote_dma(T.pb[:], T.po2[:], S.pb, S.sp2, pid, rid, off)
+
+    te.wait_ge(S["qt%d" % r], 1)
+    mm_tile(B, T.w2q, T.w2s, xcol(T.tq, r), xcol(T.ts, r), True, False)
+    for d in W_ROAD:
+        te.wait_ge(S["fw%d" % d], 4 * n2)
+        te.wait_ge(S["ft%d" % d], 2 * n2)
+        mm_tile(B, T["fw%dq" % d], T["fw%ds" % d], T["ft%dq" % d][:, 0:NC], T["ft%ds" % d][:, 0:NC], False, d == W_ROAD[-1])
+
+    ve.wait_ge(S.lw3, 16)
+    ve.quantize_mx(T.w3q[:], T.w3s[:], T.w3b[:]).then_inc(S.qw3, 1)
+    for i in range(G):
+        a = slice(NC * i, NC * i + NC)
+        ve.wait_ge(S["pa%d" % (i // 2)], noff)
+        ve.wait_ge(S["pe%d" % (B + i)], nm[B + i])
+        ve.tensor_tensor(T.u[:, a], bank(B + i), T.pa[:, a], AluOpType.add).then_inc(S["ev%d" % (B + i)], 1)
+        ne[B + i] += 1
+    ve.wait_ge(S.pb, noff)
+    for i in range(G):
+        a = slice(NC * i, NC * i + NC)
+        ve.wait_ge(S["ev%d" % (B + i)], ne[B + i])
+        ve.tensor_tensor(T.v[:, a], T.u[:, a], T.pb[:, a], AluOpType.add).then_inc(S["u%d" % i], 1)
+        ac.wait_ge(S["u%d" % i], 1)
+        ac.activation(T.hb[:, i:TW:G], T.v[:, a], RELU, scale=C2).then_inc(S.ha, 1)
+    ve.wait_ge(S.ha, G)
+    ve.quantize_mx(xcol(T.hq, r), xcol(T.hs, r), T.hb[:]).then_inc(S.qh, 1)
+    g.wait_ge(S.qh, 1)
+    gather(T.hq, T.hs, "h", S.sh)
+
+    sy.wait_ge(S.sp2, noff)
+    for c in range(N):
+        sy.wait_ge(S["qt%d" % c], 1)
+        sy.dma_start(T.t[c], T.tb[:, TW * c:TW * c + TW]).then_inc(S.st, 16)
+    stores = N
+    sy.wait_ge(S.sh, 2 * noff)
+    sy.wait_ge(S.ha, G)
+    sy.dma_start(T.h[:], T.hb[:]).then_inc(S.st, 16)
+    stores += 1
+
+    te.wait_ge(S.qw3, 1)
+    te.wait_ge(S.qh, 1)
+    for n, c in enumerate([r] + others):
+        base = (A, B)[n % 2]
+        if c != r:
+            te.wait_ge(S["h%d" % c], 2 * n4)
+        mm_tile(base, T.w3q, T.w3s, xcol(T.hq, c), xcol(T.hs, c))
+        evac(base, lambda b: T.yb[:, TW * c + NC * b:TW * c + NC * b + NC], False)
+        if n < N - 1:
+            wait_ev(sy, base)
+            sy.dma_start(T.y[:, TW * c:TW * c + TW], T.yb[:, TW * c:TW * c + TW]).then_inc(S.st, 16)
+            stores += 1
+        else:
+            w = TW // 2
+            for k in (base, base + 1):
+                sy.wait_ge(S["ev%d" % k], ne[k])
+            sy.dma_start(T.y[:, TW * c:TW * c + w], T.yb[:, TW * c:TW * c + w]).then_inc(S.st, 16)
+            stores += 1
+            for k in (base + 2, base + 3):
+                ac.wait_ge(S["ev%d" % k], ne[k])
+            ac.dma_start(T.y[:, TW * c + w:TW * c + TW], T.yb[:, TW * c + w:TW * c + TW]).then_inc(S.st2, 16)
+    sy.wait_ge(S.st, 16 * stores)
+    ac.wait_ge(S.st2, 16)
+    g.wait_ge(S.sx, 2 * noff)
+    g.wait_ge(S.sw, 2 * count(near))
+    g.wait_ge(S.sp1, count(near))
+    g.wait_ge(S.stq, 2 * noff)
+    g.wait_ge(S.sp2, noff)
+    g.wait_ge(S.sh, 2 * noff)

@@ -10,8 +10,10 @@ SIM_CORES = 96
 C1 = float(np.float32(0.047))
 C2 = float(np.float32(0.02102))
 W_ROAD = (1, 2)
-P_RELAY = 3
-P_DIRECT = 4
+P_ROAD = (3, 4)
+H_FIRST = (1, 2)
+H_HELPED = 3
+H_LAST = 4
 
 FP8 = "float8_e4m3fn_x4"
 SCRATCH = {
@@ -29,22 +31,20 @@ SCRATCH = {
     "fw2q": ("sbuf", [128, 512], FP8), "fw2s": ("sbuf", [128, 512], "uint8"),
     "ft1q": ("sbuf", [128, NC], FP8), "ft1s": ("sbuf", [128, NC], "uint8"),
     "ft2q": ("sbuf", [128, NC], FP8), "ft2s": ("sbuf", [128, NC], "uint8"),
-    "po1": ("sbuf", [128, TW], "float32"), "po2": ("sbuf", [128, TW], "float32"),
-    "pa": ("sbuf", [128, TW], "float32"), "pb": ("sbuf", [128, TW], "float32"),
+    "po0": ("sbuf", [128, TW], "float32"), "po1": ("sbuf", [128, TW], "float32"),
+    "pi0": ("sbuf", [128, TW], "float32"), "pi1": ("sbuf", [128, TW], "float32"),
     "u": ("sbuf", [128, TW], "float32"), "v": ("sbuf", [128, TW], "float32"),
     "hb": ("sbuf", [128, TW], "bfloat16"),
     "hq": ("sbuf", [128, N * NC], FP8), "hs": ("sbuf", [128, N * NC], "uint8"),
     "yb": ("sbuf", [128, N * TW], "float32"),
     "rwq": ("sbuf", [128, 256], FP8), "rws": ("sbuf", [128, 256], "uint8"),
-    "rp": ("sbuf", [128, TW // 2], "float32"),
     "ps": ("psum", [128, 4096], "float32"),
 }
 SEMAPHORES = (["lx", "lw1", "lw2", "lw3", "qx", "qw1", "qw2", "qw3", "qh", "ha", "st", "st2",
-               "sx", "sw", "sp1", "stq", "sp2", "sh", "rwc", "rwp", "rpa", "s1", "s2",
-               "fw1", "fw2", "ft1", "ft2", "pa0", "pa1", "pb"]
+               "sx", "sw", "stq", "sp0", "sp1", "sh", "rwc", "rwp", "rhc", "rhp", "s1", "s2",
+               "fw1", "fw2", "ft1", "ft2", "pi0", "pi1", "u"]
               + ["pe%d" % b for b in range(8)] + ["ev%d" % b for b in range(8)]
-              + ["qt%d" % c for c in range(N)] + ["x%d" % c for c in range(N)] + ["h%d" % c for c in range(N)]
-              + ["u%d" % i for i in range(G)])
+              + ["qt%d" % c for c in range(N)] + ["x%d" % c for c in range(N)] + ["h%d" % c for c in range(N)])
 
 
 def bits(m):
@@ -70,34 +70,39 @@ def by(v):
     return v.bitcast(dt.uint8)
 
 
+def xcol(buf, c):
+    return buf[:, NC * c:NC * c + NC]
+
+
 def helpers_of(topo, core):
     return [k for k in range(SIM_CORES) if topo.chip(k) == topo.chip(core) and topo.die(k) != topo.die(core)][:2]
+
+
+def upper(topo, core, near, far):
+    return topo.mask(core, near) & ~topo.mask(core, far)
 
 
 def helper_program(g, core, T, topo, r, half):
     S = T.sem
     dests = [T.cores[(r + d) % N] for d in W_ROAD]
     off = topo.mask(core, dests[0])
-    gm = groups(off, 2)
-    n_in = count(groups(upper(topo, T.cores[r], core, dests[0]), 2)[0])
+    off2 = groups(off, 2)
+    n_in = count(upper(topo, T.cores[r], core, dests[0]))
     a, b = 256 * half, 256 * half + 256
-    g.wait_ge(S.rwc, n_in)
-    g.remote_dma_fused([to(topo, dests[k], gm[k], S["fw%d" % W_ROAD[k]], by(T["fw%dq" % W_ROAD[k]][:, a:b]), by(T.rwq[:, 0:256]))
-                        for k in range(2)], local_sem=S.s1)
-    g.wait_ge(S.rwp, n_in)
-    g.remote_dma_fused([to(topo, dests[k], gm[k], S["fw%d" % W_ROAD[k]], T["fw%ds" % W_ROAD[k]][:, a:b], T.rws[:, 0:256])
-                        for k in range(2)], local_sem=S.s1)
-    g.wait_ge(S.rpa, n_in)
-    dst = T.cores[(r + P_RELAY) % N]
-    rid, pid, _ = topo.addr(dst)
-    w = TW // 2
-    g.remote_dma(T.pa[:, w * half:w * half + w], T.rp[:, 0:w], S["pa%d" % half], S.s2, pid, rid, topo.mask(core, dst))
+    g.wait_ge(S.rwc, n_in // 2)
+    g.remote_dma_fused([to(topo, dests[k], off2[k], S["fw%d" % d], by(T["fw%dq" % d][:, a:b]), by(T.rwq[:, 0:256]))
+                        for k, d in enumerate(W_ROAD)], local_sem=S.s1)
+    g.wait_ge(S.rwp, n_in // 2)
+    g.remote_dma_fused([to(topo, dests[k], off2[k], S["fw%d" % d], T["fw%ds" % d][:, a:b], T.rws[:, 0:256])
+                        for k, d in enumerate(W_ROAD)], local_sem=S.s1)
     g.wait_ge(S.s1, 2 * count(off))
-    g.wait_ge(S.s2, count(topo.mask(core, dst)))
-
-
-def upper(topo, core, near, far):
-    return topo.mask(core, near) & ~topo.mask(core, far)
+    if half == 0:
+        rid, pid, _ = topo.addr(T.cores[(r + H_HELPED) % N])
+        g.wait_ge(S.rhc, n_in)
+        g.remote_dma(by(xcol(T.hq, r)), by(xcol(T.hq, r)), S["h%d" % r], S.s2, pid, rid, off)
+        g.wait_ge(S.rhp, n_in)
+        g.remote_dma(xcol(T.hs, r), xcol(T.hs, r), S["h%d" % r], S.s2, pid, rid, off)
+        g.wait_ge(S.s2, 2 * count(off))
 
 
 def rank_program(g, core, T, topo):
@@ -110,11 +115,11 @@ def rank_program(g, core, T, topo):
                 helper_program(g, core, T, topo, k, hs.index(core))
         return
     helpers = helpers_of(topo, core)
-    others = [(r + d) % N for d in (1, 2, 3, 4)]
-    off = topo.mask(core, T.cores[others[0]])
-    near = upper(topo, core, helpers[0], T.cores[others[0]])
-    off4, off2, near2 = groups(off, 4), groups(off, 2), groups(near, 2)
-    n4, n2, noff = count(off4[0]), count(off2[0]), count(off)
+    q1, q2, p1, p2 = [(r + d) % N for d in W_ROAD + P_ROAD]
+    off = topo.mask(core, T.cores[q1])
+    near = upper(topo, core, helpers[0], T.cores[q1])
+    off2, near2 = groups(off, 2), groups(near, 2)
+    n2, noff = count(off2[0]), count(off)
     te, ve, ac, sy = g.tensor, g.vector, g.scalar, g.sync
     RELU, COPY = ActivationFunctionType.Relu, ActivationFunctionType.Copy
     A, B = 0, 4
@@ -146,35 +151,35 @@ def rank_program(g, core, T, topo):
             ne[k] += 1
 
     def wait_ev(q, base):
-        m = [(S["ev%d" % k], ne[k]) for k in range(base, base + G)]
-        for s, n in m:
-            q.wait_ge(s, n)
-
-    def xcol(buf, c):
-        return buf[:, NC * c:NC * c + NC]
+        for k in range(base, base + G):
+            q.wait_ge(S["ev%d" % k], ne[k])
 
     def first(base, c):
         if c != r:
-            te.wait_ge(S["x%d" % c], 2 * n4)
+            te.wait_ge(S["x%d" % c], 2 * n2)
         mm_tile(base, T.w1q, T.w1s, xcol(T.xq, c), xcol(T.xs, c))
-
-    def act_t(base, c):
         evac(base, lambda b: T.tb[:, TW * c + b:TW * c + TW:G], True)
         wait_ev(ve, base)
         ve.quantize_mx(xcol(T.tq, c), xcol(T.ts, c), T.tb[:, TW * c:TW * c + TW]).then_inc(S["qt%d" % c], 1)
 
-    def second(base, c):
+    def second(base, k, c):
+        out = T["po%d" % k]
         te.wait_ge(S["qt%d" % c], 1)
         mm_tile(base, T.w2q, T.w2s, xcol(T.tq, c), xcol(T.ts, c))
+        evac(base, lambda b: out[:, NC * b:NC * b + NC], False)
+        wait_ev(g, base)
+        rid, pid, _ = topo.addr(T.cores[c])
+        g.remote_dma(T["pi%d" % k][:], out[:], S["pi%d" % k], S["sp%d" % k], pid, rid, off)
 
-    def copy_p(base, buf):
-        evac(base, lambda b: buf[:, NC * b:NC * b + NC], False)
+    def send_all(d, src_q, src_s, dst_q, dst_s, sem, local):
+        rid, pid, _ = topo.addr(T.cores[(r + d) % N])
+        g.remote_dma(by(dst_q), by(src_q), sem, local, pid, rid, off)
+        g.remote_dma(dst_s, src_s, sem, local, pid, rid, off)
 
-    def gather(q, s, sem, local):
-        g.remote_dma_fused([to(topo, T.cores[c], off4[k], S["%s%d" % (sem, r)], by(xcol(q, r)), by(xcol(q, r)))
-                            for k, c in enumerate(others)], local_sem=local)
-        g.remote_dma_fused([to(topo, T.cores[c], off4[k], S["%s%d" % (sem, r)], xcol(s, r), xcol(s, r))
-                            for k, c in enumerate(others)], local_sem=local)
+    def send_x(offsets):
+        for f, buf in ((by, T.xq), (lambda v: v, T.xs)):
+            g.remote_dma_fused([to(topo, T.cores[(r + d) % N], off2[k], S["x%d" % r], f(xcol(buf, r)), f(xcol(buf, r)))
+                                for k, d in enumerate(offsets)], local_sem=S.sx)
 
     sy.dma_start(T.xb[:], T.x[:]).then_inc(S.lx, 16)
     sy.dma_start(T.w2b[:], T.w2[:]).then_inc(S.lw2, 16)
@@ -185,97 +190,83 @@ def rank_program(g, core, T, topo):
     ve.quantize_mx(T.w2q[:], T.w2s[:], T.w2b[:]).then_inc(S.qw2, 1)
     ve.wait_ge(S.lw1, 16)
     ve.quantize_mx(T.w1q[:], T.w1s[:], T.w1b[:]).then_inc(S.qw1, 1)
-
     g.wait_ge(S.qx, 1)
-    gather(T.xq, T.xs, "x", S.sx)
+    send_x([N - d for d in P_ROAD])
     g.wait_ge(S.qw2, 1)
     g.remote_dma_fused([to(topo, helpers[k], near2[k], S.rwc, by(T.rwq[:, 0:256]), by(T.w2q[:, 256 * k:256 * k + 256])) for k in range(2)],
                        local_sem=S.sw)
     g.remote_dma_fused([to(topo, helpers[k], near2[k], S.rwp, T.rws[:, 0:256], T.w2s[:, 256 * k:256 * k + 256]) for k in range(2)],
                        local_sem=S.sw)
-    sy.wait_ge(S.sx, 2 * noff)
+    send_x([N - d for d in W_ROAD])
+    sy.wait_ge(S.sx, 4 * noff)
     sy.dma_start(T.w3b[:], T.w3[:]).then_inc(S.lw3, 16)
 
-    q1, q2, p1, p2 = [(r + d) % N for d in (W_ROAD[0], W_ROAD[1], P_RELAY, P_DIRECT)]
     te.wait_ge(S.qx, 1)
     te.wait_ge(S.qw1, 1)
     first(A, r)
-    act_t(A, r)
     first(B, p1)
-    act_t(B, p1)
-    first(A, q1)
-    act_t(A, q1)
+    first(A, p2)
     te.wait_ge(S.qw2, 1)
-    second(B, p1)
-    copy_p(B, T.po1)
-    wait_ev(g, B)
-    g.remote_dma_fused([to(topo, helpers[k], near2[k], S.rpa, T.rp[:, 0:TW // 2], T.po1[:, TW // 2 * k:TW // 2 * k + TW // 2])
-                        for k in range(2)], local_sem=S.sp1)
-    first(A, q2)
-    act_t(A, q2)
-    g.wait_ge(S["qt%d" % q1], 1)
-    g.wait_ge(S["qt%d" % q2], 1)
-    g.remote_dma_fused([to(topo, T.cores[c], off2[k], S["ft%d" % W_ROAD[k]], by(T["ft%dq" % W_ROAD[k]][:, 0:NC]), by(xcol(T.tq, c)))
-                        for k, c in enumerate((q1, q2))], local_sem=S.stq)
-    g.remote_dma_fused([to(topo, T.cores[c], off2[k], S["ft%d" % W_ROAD[k]], T["ft%ds" % W_ROAD[k]][:, 0:NC], xcol(T.ts, c))
-                        for k, c in enumerate((q1, q2))], local_sem=S.stq)
-    first(B, p2)
-    act_t(B, p2)
-    second(A, p2)
-    copy_p(A, T.po2)
-    wait_ev(g, A)
-    rid, pid, _ = topo.addr(T.cores[p2])
-    g.remote_dma(T.pb[:], T.po2[:], S.pb, S.sp2, pid, rid, off)
+    second(B, 0, p1)
+    second(A, 1, p2)
+    for base, d, c in ((B, W_ROAD[0], q1), (A, W_ROAD[1], q2)):
+        first(base, c)
+        g.wait_ge(S["qt%d" % c], 1)
+        send_all(d, xcol(T.tq, c), xcol(T.ts, c), T["ft%dq" % d][:], T["ft%ds" % d][:], S["ft%d" % d], S.stq)
 
     te.wait_ge(S["qt%d" % r], 1)
     mm_tile(B, T.w2q, T.w2s, xcol(T.tq, r), xcol(T.ts, r), True, False)
     for d in W_ROAD:
         te.wait_ge(S["fw%d" % d], 4 * n2)
-        te.wait_ge(S["ft%d" % d], 2 * n2)
-        mm_tile(B, T["fw%dq" % d], T["fw%ds" % d], T["ft%dq" % d][:, 0:NC], T["ft%ds" % d][:, 0:NC], False, d == W_ROAD[-1])
-
+        te.wait_ge(S["ft%d" % d], 2 * noff)
+        mm_tile(B, T["fw%dq" % d], T["fw%ds" % d], T["ft%dq" % d][:], T["ft%ds" % d][:], False, d == W_ROAD[-1])
     ve.wait_ge(S.lw3, 16)
     ve.quantize_mx(T.w3q[:], T.w3s[:], T.w3b[:]).then_inc(S.qw3, 1)
+    ve.wait_ge(S.pi0, noff)
+    ve.wait_ge(S.pi1, noff)
+    ve.tensor_tensor(T.u[:], T.pi0[:], T.pi1[:], AluOpType.add).then_inc(S.u, 1)
+    ve.wait_ge(S.u, 1)
     for i in range(G):
-        a = slice(NC * i, NC * i + NC)
-        ve.wait_ge(S["pa%d" % (i // 2)], noff)
-        ve.wait_ge(S["pe%d" % (B + i)], nm[B + i])
-        ve.tensor_tensor(T.u[:, a], bank(B + i), T.pa[:, a], AluOpType.add).then_inc(S["ev%d" % (B + i)], 1)
-        ne[B + i] += 1
-    ve.wait_ge(S.pb, noff)
-    for i in range(G):
-        a = slice(NC * i, NC * i + NC)
-        ve.wait_ge(S["ev%d" % (B + i)], ne[B + i])
-        ve.tensor_tensor(T.v[:, a], T.u[:, a], T.pb[:, a], AluOpType.add).then_inc(S["u%d" % i], 1)
-        ac.wait_ge(S["u%d" % i], 1)
+        a, k = slice(NC * i, NC * i + NC), B + i
+        ve.wait_ge(S["pe%d" % k], nm[k])
+        ve.tensor_tensor(T.v[:, a], bank(k), T.u[:, a], AluOpType.add).then_inc(S["ev%d" % k], 1)
+        ne[k] += 1
+        ac.wait_ge(S["ev%d" % k], ne[k])
         ac.activation(T.hb[:, i:TW:G], T.v[:, a], RELU, scale=C2).then_inc(S.ha, 1)
     ve.wait_ge(S.ha, G)
     ve.quantize_mx(xcol(T.hq, r), xcol(T.hs, r), T.hb[:]).then_inc(S.qh, 1)
     g.wait_ge(S.qh, 1)
-    gather(T.hq, T.hs, "h", S.sh)
+    for f, buf, sem in ((by, T.hq, S.rhc), (lambda v: v, T.hs, S.rhp)):
+        g.remote_dma_fused([to(topo, helpers[0], near, sem, f(xcol(buf, r)), f(xcol(buf, r)))]
+                           + [to(topo, T.cores[(r + d) % N], off2[k], S["h%d" % r], f(xcol(buf, r)), f(xcol(buf, r)))
+                              for k, d in enumerate(H_FIRST)], local_sem=S.sh)
+    send_all(H_LAST, xcol(T.hq, r), xcol(T.hs, r), xcol(T.hq, r), xcol(T.hs, r), S["h%d" % r], S.sh)
 
-    sy.wait_ge(S.sp2, noff)
+    sy.wait_ge(S.sp0, noff)
+    sy.wait_ge(S.sp1, noff)
+    sy.wait_ge(S.stq, 4 * noff)
     for c in range(N):
         sy.wait_ge(S["qt%d" % c], 1)
         sy.dma_start(T.t[c], T.tb[:, TW * c:TW * c + TW]).then_inc(S.st, 16)
     stores = N
-    sy.wait_ge(S.sh, 2 * noff)
-    sy.wait_ge(S.ha, G)
-    sy.dma_start(T.h[:], T.hb[:]).then_inc(S.st, 16)
-    stores += 1
 
     te.wait_ge(S.qw3, 1)
     te.wait_ge(S.qh, 1)
-    for n, c in enumerate([r] + others):
+    for n, d in enumerate((0,) + H_FIRST + (H_LAST, H_HELPED)):
+        c = (r - d) % N
         base = (A, B)[n % 2]
-        if c != r:
-            te.wait_ge(S["h%d" % c], 2 * n4)
+        if d:
+            te.wait_ge(S["h%d" % c], 2 * n2 if d in H_FIRST else 2 * noff)
         mm_tile(base, T.w3q, T.w3s, xcol(T.hq, c), xcol(T.hs, c))
         evac(base, lambda b: T.yb[:, TW * c + NC * b:TW * c + NC * b + NC], False)
         if n < N - 1:
             wait_ev(sy, base)
             sy.dma_start(T.y[:, TW * c:TW * c + TW], T.yb[:, TW * c:TW * c + TW]).then_inc(S.st, 16)
             stores += 1
+            if d == 0:
+                sy.wait_ge(S.ha, G)
+                sy.dma_start(T.h[:], T.hb[:]).then_inc(S.st, 16)
+                stores += 1
         else:
             w = TW // 2
             for k in (base, base + 1):
@@ -287,9 +278,9 @@ def rank_program(g, core, T, topo):
             ac.dma_start(T.y[:, TW * c + w:TW * c + TW], T.yb[:, TW * c + w:TW * c + TW]).then_inc(S.st2, 16)
     sy.wait_ge(S.st, 16 * stores)
     ac.wait_ge(S.st2, 16)
-    g.wait_ge(S.sx, 2 * noff)
+    g.wait_ge(S.sx, 4 * noff)
     g.wait_ge(S.sw, 2 * count(near))
-    g.wait_ge(S.sp1, count(near))
-    g.wait_ge(S.stq, 2 * noff)
-    g.wait_ge(S.sp2, noff)
-    g.wait_ge(S.sh, 2 * noff)
+    g.wait_ge(S.sp0, noff)
+    g.wait_ge(S.sp1, noff)
+    g.wait_ge(S.stq, 4 * noff)
+    g.wait_ge(S.sh, 4 * noff + 2 * count(near))

@@ -10,10 +10,11 @@ SIM_CORES = 96
 C1 = float(np.float32(0.047))
 C2 = float(np.float32(0.02102))
 W_ROAD = (1, 2)
+T_HELPED = 1
 P_ROAD = (3, 4)
-H_FIRST = (1, 2)
+H_FIRST = 1
 H_HELPED = 3
-H_LAST = 4
+H_NEXT = (2, 4)
 
 FP8 = "float8_e4m3fn_x4"
 SCRATCH = {
@@ -38,12 +39,13 @@ SCRATCH = {
     "hq": ("sbuf", [128, N * NC], FP8), "hs": ("sbuf", [128, N * NC], "uint8"),
     "yb": ("sbuf", [128, N * TW], "float32"),
     "rwq": ("sbuf", [128, 256], FP8), "rws": ("sbuf", [128, 256], "uint8"),
+    "rtq": ("sbuf", [128, NC], FP8), "rts": ("sbuf", [128, NC], "uint8"),
     "ps": ("psum", [128, 4096], "float32"),
 }
 SEMAPHORES = (["lx", "lw1", "lw2", "lw3", "qx", "qw1", "qw2", "qw3", "qh", "ha", "st", "st2",
-               "sx", "sw", "stq", "sp0", "sp1", "sh", "rwc", "rwp", "rhc", "rhp", "s1", "s2",
-               "fw1", "fw2", "ft1", "ft2", "pi0", "pi1", "u"]
-              + ["pe%d" % b for b in range(8)] + ["ev%d" % b for b in range(8)]
+               "sx", "sw", "stq", "sp0", "sp1", "sh", "rwc", "rwp", "rtc", "rtp", "rhc", "rhp", "s1", "s2", "s3",
+               "fw1", "fw2", "ft1", "ft2", "pi0", "pi1"]
+              + ["pe%d" % b for b in range(8)] + ["ev%d" % b for b in range(8)] + ["u%d" % b for b in range(G)]
               + ["qt%d" % c for c in range(N)] + ["x%d" % c for c in range(N)] + ["h%d" % c for c in range(N)])
 
 
@@ -89,20 +91,28 @@ def helper_program(g, core, T, topo, r, half):
     off2 = groups(off, 2)
     n_in = count(upper(topo, T.cores[r], core, dests[0]))
     a, b = 256 * half, 256 * half + 256
-    g.wait_ge(S.rwc, n_in // 2)
-    g.remote_dma_fused([to(topo, dests[k], off2[k], S["fw%d" % d], by(T["fw%dq" % d][:, a:b]), by(T.rwq[:, 0:256]))
-                        for k, d in enumerate(W_ROAD)], local_sem=S.s1)
     g.wait_ge(S.rwp, n_in // 2)
     g.remote_dma_fused([to(topo, dests[k], off2[k], S["fw%d" % d], T["fw%ds" % d][:, a:b], T.rws[:, 0:256])
                         for k, d in enumerate(W_ROAD)], local_sem=S.s1)
-    g.wait_ge(S.s1, 2 * count(off))
-    if half == 0:
+    g.wait_ge(S.rwc, n_in // 2)
+    g.remote_dma_fused([to(topo, dests[k], off2[k], S["fw%d" % d], by(T["fw%dq" % d][:, a:b]), by(T.rwq[:, 0:256]))
+                        for k, d in enumerate(W_ROAD)], local_sem=S.s1)
+    if half == 1:
+        d = T_HELPED
+        rid, pid, _ = topo.addr(T.cores[(r + d) % N])
+        g.wait_ge(S.rtc, n_in)
+        g.remote_dma(by(T["ft%dq" % d][:]), by(T.rtq[:]), S["ft%d" % d], S.s3, pid, rid, off)
+        g.wait_ge(S.rtp, n_in)
+        g.remote_dma(T["ft%ds" % d][:], T.rts[:], S["ft%d" % d], S.s3, pid, rid, off)
+        g.wait_ge(S.s3, 2 * count(off))
+    else:
         rid, pid, _ = topo.addr(T.cores[(r + H_HELPED) % N])
         g.wait_ge(S.rhc, n_in)
         g.remote_dma(by(xcol(T.hq, r)), by(xcol(T.hq, r)), S["h%d" % r], S.s2, pid, rid, off)
         g.wait_ge(S.rhp, n_in)
         g.remote_dma(xcol(T.hs, r), xcol(T.hs, r), S["h%d" % r], S.s2, pid, rid, off)
         g.wait_ge(S.s2, 2 * count(off))
+    g.wait_ge(S.s1, 2 * count(off))
 
 
 def rank_program(g, core, T, topo):
@@ -156,7 +166,7 @@ def rank_program(g, core, T, topo):
 
     def first(base, c):
         if c != r:
-            te.wait_ge(S["x%d" % c], 2 * n2)
+            te.wait_ge(S["x%d" % c], 2 * noff)
         mm_tile(base, T.w1q, T.w1s, xcol(T.xq, c), xcol(T.xs, c))
         evac(base, lambda b: T.tb[:, TW * c + b:TW * c + TW:G], True)
         wait_ev(ve, base)
@@ -171,15 +181,22 @@ def rank_program(g, core, T, topo):
         rid, pid, _ = topo.addr(T.cores[c])
         g.remote_dma(T["pi%d" % k][:], out[:], S["pi%d" % k], S["sp%d" % k], pid, rid, off)
 
-    def send_all(d, src_q, src_s, dst_q, dst_s, sem, local):
-        rid, pid, _ = topo.addr(T.cores[(r + d) % N])
-        g.remote_dma(by(dst_q), by(src_q), sem, local, pid, rid, off)
-        g.remote_dma(dst_s, src_s, sem, local, pid, rid, off)
+    def send(dst, mask, src_q, src_s, dst_q, dst_s, sem_q, sem_s, local):
+        rid, pid, _ = topo.addr(dst)
+        g.remote_dma(by(dst_q), by(src_q), sem_q, local, pid, rid, mask)
+        g.remote_dma(dst_s, src_s, sem_s, local, pid, rid, mask)
 
-    def send_x(offsets):
-        for f, buf in ((by, T.xq), (lambda v: v, T.xs)):
-            g.remote_dma_fused([to(topo, T.cores[(r + d) % N], off2[k], S["x%d" % r], f(xcol(buf, r)), f(xcol(buf, r)))
-                                for k, d in enumerate(offsets)], local_sem=S.sx)
+    def send_slot(name, d, local):
+        q, s, sem = xcol(T[name + "q"], r), xcol(T[name + "s"], r), S["%s%d" % (name, r)]
+        send(T.cores[(r + d) % N], off, q, s, q, s, sem, sem, local)
+
+    def send_t(d, c):
+        g.wait_ge(S["qt%d" % c], 1)
+        q, s = xcol(T.tq, c), xcol(T.ts, c)
+        if d == T_HELPED:
+            send(helpers[1], near, q, s, T.rtq[:], T.rts[:], S.rtc, S.rtp, S.stq)
+        else:
+            send(T.cores[c], off, q, s, T["ft%dq" % d][:], T["ft%ds" % d][:], S["ft%d" % d], S["ft%d" % d], S.stq)
 
     sy.dma_start(T.xb[:], T.x[:]).then_inc(S.lx, 16)
     sy.dma_start(T.w2b[:], T.w2[:]).then_inc(S.lw2, 16)
@@ -191,28 +208,30 @@ def rank_program(g, core, T, topo):
     ve.wait_ge(S.lw1, 16)
     ve.quantize_mx(T.w1q[:], T.w1s[:], T.w1b[:]).then_inc(S.qw1, 1)
     g.wait_ge(S.qx, 1)
-    send_x([N - d for d in P_ROAD])
+    for d in P_ROAD:
+        send_slot("x", N - d, S.sx)
     g.wait_ge(S.qw2, 1)
-    g.remote_dma_fused([to(topo, helpers[k], near2[k], S.rwc, by(T.rwq[:, 0:256]), by(T.w2q[:, 256 * k:256 * k + 256])) for k in range(2)],
-                       local_sem=S.sw)
     g.remote_dma_fused([to(topo, helpers[k], near2[k], S.rwp, T.rws[:, 0:256], T.w2s[:, 256 * k:256 * k + 256]) for k in range(2)],
                        local_sem=S.sw)
-    send_x([N - d for d in W_ROAD])
-    sy.wait_ge(S.sx, 4 * noff)
+    g.remote_dma_fused([to(topo, helpers[k], near2[k], S.rwc, by(T.rwq[:, 0:256]), by(T.w2q[:, 256 * k:256 * k + 256])) for k in range(2)],
+                       local_sem=S.sw)
+    for d in W_ROAD:
+        send_slot("x", N - d, S.sx)
+    sy.wait_ge(S.sx, 8 * noff)
     sy.dma_start(T.w3b[:], T.w3[:]).then_inc(S.lw3, 16)
 
     te.wait_ge(S.qx, 1)
     te.wait_ge(S.qw1, 1)
     first(A, r)
     first(B, p1)
-    first(A, p2)
     te.wait_ge(S.qw2, 1)
-    second(B, 0, p1)
-    second(A, 1, p2)
-    for base, d, c in ((B, W_ROAD[0], q1), (A, W_ROAD[1], q2)):
-        first(base, c)
-        g.wait_ge(S["qt%d" % c], 1)
-        send_all(d, xcol(T.tq, c), xcol(T.ts, c), T["ft%dq" % d][:], T["ft%ds" % d][:], S["ft%d" % d], S.stq)
+    second(A, 0, p1)
+    first(B, p2)
+    first(A, q1)
+    second(B, 1, p2)
+    send_t(W_ROAD[0], q1)
+    first(A, q2)
+    send_t(W_ROAD[1], q2)
 
     te.wait_ge(S["qt%d" % r], 1)
     mm_tile(B, T.w2q, T.w2s, xcol(T.tq, r), xcol(T.ts, r), True, False)
@@ -224,10 +243,12 @@ def rank_program(g, core, T, topo):
     ve.quantize_mx(T.w3q[:], T.w3s[:], T.w3b[:]).then_inc(S.qw3, 1)
     ve.wait_ge(S.pi0, noff)
     ve.wait_ge(S.pi1, noff)
-    ve.tensor_tensor(T.u[:], T.pi0[:], T.pi1[:], AluOpType.add).then_inc(S.u, 1)
-    ve.wait_ge(S.u, 1)
+    for i in range(G):
+        a = slice(NC * i, NC * i + NC)
+        ve.tensor_tensor(T.u[:, a], T.pi0[:, a], T.pi1[:, a], AluOpType.add).then_inc(S["u%d" % i], 1)
     for i in range(G):
         a, k = slice(NC * i, NC * i + NC), B + i
+        ve.wait_ge(S["u%d" % i], 1)
         ve.wait_ge(S["pe%d" % k], nm[k])
         ve.tensor_tensor(T.v[:, a], bank(k), T.u[:, a], AluOpType.add).then_inc(S["ev%d" % k], 1)
         ne[k] += 1
@@ -237,14 +258,14 @@ def rank_program(g, core, T, topo):
     ve.quantize_mx(xcol(T.hq, r), xcol(T.hs, r), T.hb[:]).then_inc(S.qh, 1)
     g.wait_ge(S.qh, 1)
     for f, buf, sem in ((by, T.hq, S.rhc), (lambda v: v, T.hs, S.rhp)):
-        g.remote_dma_fused([to(topo, helpers[0], near, sem, f(xcol(buf, r)), f(xcol(buf, r)))]
-                           + [to(topo, T.cores[(r + d) % N], off2[k], S["h%d" % r], f(xcol(buf, r)), f(xcol(buf, r)))
-                              for k, d in enumerate(H_FIRST)], local_sem=S.sh)
-    send_all(H_LAST, xcol(T.hq, r), xcol(T.hs, r), xcol(T.hq, r), xcol(T.hs, r), S["h%d" % r], S.sh)
+        g.remote_dma_fused([to(topo, helpers[0], near, sem, f(xcol(buf, r)), f(xcol(buf, r))),
+                            to(topo, T.cores[(r + H_FIRST) % N], off, S["h%d" % r], f(xcol(buf, r)), f(xcol(buf, r)))], local_sem=S.sh)
+    for d in H_NEXT:
+        send_slot("h", d, S.sh)
 
     sy.wait_ge(S.sp0, noff)
     sy.wait_ge(S.sp1, noff)
-    sy.wait_ge(S.stq, 4 * noff)
+    sy.wait_ge(S.stq, 2 * noff + 2 * count(near))
     for c in range(N):
         sy.wait_ge(S["qt%d" % c], 1)
         sy.dma_start(T.t[c], T.tb[:, TW * c:TW * c + TW]).then_inc(S.st, 16)
@@ -252,14 +273,14 @@ def rank_program(g, core, T, topo):
 
     te.wait_ge(S.qw3, 1)
     te.wait_ge(S.qh, 1)
-    for n, d in enumerate((0,) + H_FIRST + (H_LAST, H_HELPED)):
+    for d in range(N):
         c = (r - d) % N
-        base = (A, B)[n % 2]
+        base = (A, B)[d % 2]
         if d:
-            te.wait_ge(S["h%d" % c], 2 * n2 if d in H_FIRST else 2 * noff)
+            te.wait_ge(S["h%d" % c], 2 * noff)
         mm_tile(base, T.w3q, T.w3s, xcol(T.hq, c), xcol(T.hs, c))
         evac(base, lambda b: T.yb[:, TW * c + NC * b:TW * c + NC * b + NC], False)
-        if n < N - 1:
+        if d < N - 1:
             wait_ev(sy, base)
             sy.dma_start(T.y[:, TW * c:TW * c + TW], T.yb[:, TW * c:TW * c + TW]).then_inc(S.st, 16)
             stores += 1
@@ -278,9 +299,9 @@ def rank_program(g, core, T, topo):
             ac.dma_start(T.y[:, TW * c + w:TW * c + TW], T.yb[:, TW * c + w:TW * c + TW]).then_inc(S.st2, 16)
     sy.wait_ge(S.st, 16 * stores)
     ac.wait_ge(S.st2, 16)
-    g.wait_ge(S.sx, 4 * noff)
+    g.wait_ge(S.sx, 8 * noff)
     g.wait_ge(S.sw, 2 * count(near))
     g.wait_ge(S.sp0, noff)
     g.wait_ge(S.sp1, noff)
-    g.wait_ge(S.stq, 4 * noff)
-    g.wait_ge(S.sh, 4 * noff + 2 * count(near))
+    g.wait_ge(S.stq, 2 * noff + 2 * count(near))
+    g.wait_ge(S.sh, 6 * noff + 2 * count(near))

@@ -10,11 +10,12 @@ SIM_CORES = 96
 C1 = float(np.float32(0.047))
 C2 = float(np.float32(0.02102))
 W_ROAD = (1, 2)
-T_HELPED = 1
+T_HELPER = (0, 1)
 P_ROAD = (3, 4)
-H_FIRST = 1
-H_HELPED = 3
-H_NEXT = (2, 4)
+P_PIECES = (((0, 1), (1, 4)), ((0, 1), (1, 3), (3, 4)))
+X_ORDER = (3, 1, 4, 2)
+H_DIRECT = (1, 2)
+H_HELPED = (3, 4)
 
 FP8 = "float8_e4m3fn_x4"
 SCRATCH = {
@@ -42,9 +43,10 @@ SCRATCH = {
     "rtq": ("sbuf", [128, NC], FP8), "rts": ("sbuf", [128, NC], "uint8"),
     "ps": ("psum", [128, 4096], "float32"),
 }
-SEMAPHORES = (["lx", "lw1", "lw2", "lw3", "qx", "qw1", "qw2", "qw3", "qh", "ha", "st", "st2",
+SEMAPHORES = (["lx", "lw1", "lw3", "lw20", "lw21", "qw20", "qw21", "qx", "qw1", "qw3", "qh", "ha", "st", "st2",
                "sx", "sw", "stq", "sp0", "sp1", "sh", "rwc", "rwp", "rtc", "rtp", "rhc", "rhp", "s1", "s2", "s3",
-               "fw1", "fw2", "ft1", "ft2", "pi0", "pi1"]
+               "fw1", "fw2", "ft1", "ft2"]
+              + ["pi%d%d" % (k, j) for k in range(2) for j in range(len(P_PIECES[k]))]
               + ["pe%d" % b for b in range(8)] + ["ev%d" % b for b in range(8)] + ["u%d" % b for b in range(G)]
               + ["qt%d" % c for c in range(N)] + ["x%d" % c for c in range(N)] + ["h%d" % c for c in range(N)])
 
@@ -89,30 +91,32 @@ def helper_program(g, core, T, topo, r, half):
     dests = [T.cores[(r + d) % N] for d in W_ROAD]
     off = topo.mask(core, dests[0])
     off2 = groups(off, 2)
-    n_in = count(upper(topo, T.cores[r], core, dests[0]))
+    n_in, noff = count(upper(topo, T.cores[r], core, dests[0])), count(off)
     a, b = 256 * half, 256 * half + 256
-    g.wait_ge(S.rwp, n_in // 2)
+    g.wait_ge(S.rwp, n_in)
     g.remote_dma_fused([to(topo, dests[k], off2[k], S["fw%d" % d], T["fw%ds" % d][:, a:b], T.rws[:, 0:256])
                         for k, d in enumerate(W_ROAD)], local_sem=S.s1)
-    g.wait_ge(S.rwc, n_in // 2)
+    g.wait_ge(S.rwc, n_in)
     g.remote_dma_fused([to(topo, dests[k], off2[k], S["fw%d" % d], by(T["fw%dq" % d][:, a:b]), by(T.rwq[:, 0:256]))
                         for k, d in enumerate(W_ROAD)], local_sem=S.s1)
-    if half == 1:
-        d = T_HELPED
-        rid, pid, _ = topo.addr(T.cores[(r + d) % N])
-        g.wait_ge(S.rtc, n_in)
-        g.remote_dma(by(T["ft%dq" % d][:]), by(T.rtq[:]), S["ft%d" % d], S.s3, pid, rid, off)
-        g.wait_ge(S.rtp, n_in)
-        g.remote_dma(T["ft%ds" % d][:], T.rts[:], S["ft%d" % d], S.s3, pid, rid, off)
-        g.wait_ge(S.s3, 2 * count(off))
-    else:
-        rid, pid, _ = topo.addr(T.cores[(r + H_HELPED) % N])
-        g.wait_ge(S.rhc, n_in)
-        g.remote_dma(by(xcol(T.hq, r)), by(xcol(T.hq, r)), S["h%d" % r], S.s2, pid, rid, off)
-        g.wait_ge(S.rhp, n_in)
-        g.remote_dma(xcol(T.hs, r), xcol(T.hs, r), S["h%d" % r], S.s2, pid, rid, off)
-        g.wait_ge(S.s2, 2 * count(off))
-    g.wait_ge(S.s1, 2 * count(off))
+    d = W_ROAD[T_HELPER.index(half)]
+    rid, pid, _ = topo.addr(T.cores[(r + d) % N])
+    g.wait_ge(S.rtc, n_in)
+    g.remote_dma(by(T["ft%dq" % d][:]), by(T.rtq[:]), S["ft%d" % d], S.s3, pid, rid, off)
+    g.wait_ge(S.rtp, n_in)
+    g.remote_dma(T["ft%ds" % d][:], T.rts[:], S["ft%d" % d], S.s3, pid, rid, off)
+    if half == 0:
+        for k, d in enumerate(H_HELPED):
+            rid, pid, _ = topo.addr(T.cores[(r + d) % N])
+            if k == 0:
+                g.wait_ge(S.rhc, n_in)
+            g.remote_dma(by(xcol(T.hq, r)), by(xcol(T.hq, r)), S["h%d" % r], S.s2, pid, rid, off)
+            if k == 0:
+                g.wait_ge(S.rhp, n_in)
+            g.remote_dma(xcol(T.hs, r), xcol(T.hs, r), S["h%d" % r], S.s2, pid, rid, off)
+        g.wait_ge(S.s2, 2 * len(H_HELPED) * noff)
+    g.wait_ge(S.s3, 2 * noff)
+    g.wait_ge(S.s1, 2 * noff)
 
 
 def rank_program(g, core, T, topo):
@@ -128,12 +132,12 @@ def rank_program(g, core, T, topo):
     q1, q2, p1, p2 = [(r + d) % N for d in W_ROAD + P_ROAD]
     off = topo.mask(core, T.cores[q1])
     near = upper(topo, core, helpers[0], T.cores[q1])
-    off2, near2 = groups(off, 2), groups(near, 2)
-    n2, noff = count(off2[0]), count(off)
+    noff, nnear = count(off), count(near)
     te, ve, ac, sy = g.tensor, g.vector, g.scalar, g.sync
     RELU, COPY = ActivationFunctionType.Relu, ActivationFunctionType.Copy
     A, B = 0, 4
     nm, ne = [0] * 8, [0] * 8
+    sent = {"sx": 0, "sw": 0, "stq": 0, "sp0": 0, "sp1": 0, "sh": 0}
 
     def bank(k):
         return T.ps[:, 512 * k:512 * k + NC]
@@ -160,8 +164,8 @@ def rank_program(g, core, T, topo):
             ins.then_inc(S["ev%d" % k], 1)
             ne[k] += 1
 
-    def wait_ev(q, base):
-        for k in range(base, base + G):
+    def wait_ev(q, base, b0=0, b1=G):
+        for k in range(base + b0, base + b1):
             q.wait_ge(S["ev%d" % k], ne[k])
 
     def first(base, c):
@@ -172,79 +176,85 @@ def rank_program(g, core, T, topo):
         wait_ev(ve, base)
         ve.quantize_mx(xcol(T.tq, c), xcol(T.ts, c), T.tb[:, TW * c:TW * c + TW]).then_inc(S["qt%d" % c], 1)
 
+    def send(dst, dst_ap, src_ap, sem, local, mask):
+        rid, pid, _ = topo.addr(dst)
+        g.remote_dma(dst_ap, src_ap, sem, S[local], pid, rid, mask)
+        sent[local] += count(mask)
+
     def second(base, k, c):
         out = T["po%d" % k]
         te.wait_ge(S["qt%d" % c], 1)
         mm_tile(base, T.w2q, T.w2s, xcol(T.tq, c), xcol(T.ts, c))
         evac(base, lambda b: out[:, NC * b:NC * b + NC], False)
-        wait_ev(g, base)
-        rid, pid, _ = topo.addr(T.cores[c])
-        g.remote_dma(T["pi%d" % k][:], out[:], S["pi%d" % k], S["sp%d" % k], pid, rid, off)
+        for j, (b0, b1) in enumerate(P_PIECES[k]):
+            wait_ev(g, base, b0, b1)
+            w = slice(NC * b0, NC * b1)
+            send(T.cores[c], T["pi%d" % k][:, w], out[:, w], S["pi%d%d" % (k, j)], "sp%d" % k, off)
 
-    def send(dst, mask, src_q, src_s, dst_q, dst_s, sem_q, sem_s, local):
-        rid, pid, _ = topo.addr(dst)
-        g.remote_dma(by(dst_q), by(src_q), sem_q, local, pid, rid, mask)
-        g.remote_dma(dst_s, src_s, sem_s, local, pid, rid, mask)
-
-    def send_slot(name, d, local):
+    def send_slot(name, d, local, plane_first=False):
         q, s, sem = xcol(T[name + "q"], r), xcol(T[name + "s"], r), S["%s%d" % (name, r)]
-        send(T.cores[(r + d) % N], off, q, s, q, s, sem, sem, local)
+        for v in ((s, by(q)) if plane_first else (by(q), s)):
+            send(T.cores[(r + d) % N], v, v, sem, local, off)
 
-    def send_t(d, c):
+    def send_w2(k):
+        a = slice(256 * k, 256 * k + 256)
+        g.wait_ge(S["qw2%d" % k], 1)
+        send(helpers[k], T.rws[:, 0:256], T.w2s[:, a], S.rwp, "sw", near)
+        send(helpers[k], by(T.rwq[:, 0:256]), by(T.w2q[:, a]), S.rwc, "sw", near)
+
+    def send_t(k, c):
         g.wait_ge(S["qt%d" % c], 1)
-        q, s = xcol(T.tq, c), xcol(T.ts, c)
-        if d == T_HELPED:
-            send(helpers[1], near, q, s, T.rtq[:], T.rts[:], S.rtc, S.rtp, S.stq)
-        else:
-            send(T.cores[c], off, q, s, T["ft%dq" % d][:], T["ft%ds" % d][:], S["ft%d" % d], S["ft%d" % d], S.stq)
+        send(helpers[T_HELPER[k]], by(T.rtq[:]), by(xcol(T.tq, c)), S.rtc, "stq", near)
+        send(helpers[T_HELPER[k]], T.rts[:], xcol(T.ts, c), S.rtp, "stq", near)
 
     sy.dma_start(T.xb[:], T.x[:]).then_inc(S.lx, 16)
-    sy.dma_start(T.w2b[:], T.w2[:]).then_inc(S.lw2, 16)
+    for k in range(2):
+        sy.dma_start(T.w2b[:, 1024 * k:1024 * k + 1024], T.w2[:, 1024 * k:1024 * k + 1024]).then_inc(S["lw2%d" % k], 16)
     sy.dma_start(T.w1b[:], T.w1[:]).then_inc(S.lw1, 16)
     ve.wait_ge(S.lx, 16)
     ve.quantize_mx(xcol(T.xq, r), xcol(T.xs, r), T.xb[:]).then_inc(S.qx, 1)
-    ve.wait_ge(S.lw2, 16)
-    ve.quantize_mx(T.w2q[:], T.w2s[:], T.w2b[:]).then_inc(S.qw2, 1)
+    for k in range(2):
+        a = slice(256 * k, 256 * k + 256)
+        ve.wait_ge(S["lw2%d" % k], 16)
+        ve.quantize_mx(T.w2q[:, a], T.w2s[:, a], T.w2b[:, 1024 * k:1024 * k + 1024]).then_inc(S["qw2%d" % k], 1)
     ve.wait_ge(S.lw1, 16)
     ve.quantize_mx(T.w1q[:], T.w1s[:], T.w1b[:]).then_inc(S.qw1, 1)
     g.wait_ge(S.qx, 1)
-    for d in P_ROAD:
-        send_slot("x", N - d, S.sx)
-    g.wait_ge(S.qw2, 1)
-    g.remote_dma_fused([to(topo, helpers[k], near2[k], S.rwp, T.rws[:, 0:256], T.w2s[:, 256 * k:256 * k + 256]) for k in range(2)],
-                       local_sem=S.sw)
-    g.remote_dma_fused([to(topo, helpers[k], near2[k], S.rwc, by(T.rwq[:, 0:256]), by(T.w2q[:, 256 * k:256 * k + 256])) for k in range(2)],
-                       local_sem=S.sw)
-    for d in W_ROAD:
-        send_slot("x", N - d, S.sx)
-    sy.wait_ge(S.sx, 8 * noff)
+    for i, d in enumerate(X_ORDER):
+        send_slot("x", N - d, "sx", i == 0)
+        if i < 2:
+            send_w2(i)
+    sy.wait_ge(S["x%d" % p1], 2 * noff)
     sy.dma_start(T.w3b[:], T.w3[:]).then_inc(S.lw3, 16)
 
     te.wait_ge(S.qx, 1)
     te.wait_ge(S.qw1, 1)
     first(A, r)
     first(B, p1)
-    te.wait_ge(S.qw2, 1)
-    second(A, 0, p1)
-    first(B, p2)
     first(A, q1)
-    second(B, 1, p2)
-    send_t(W_ROAD[0], q1)
-    first(A, q2)
-    send_t(W_ROAD[1], q2)
+    te.wait_ge(S.qw20, 1)
+    te.wait_ge(S.qw21, 1)
+    second(B, 0, p1)
+    send_t(0, q1)
+    first(A, p2)
+    first(B, q2)
+    send_t(1, q2)
+    second(A, 1, p2)
 
     te.wait_ge(S["qt%d" % r], 1)
     mm_tile(B, T.w2q, T.w2s, xcol(T.tq, r), xcol(T.ts, r), True, False)
     for d in W_ROAD:
-        te.wait_ge(S["fw%d" % d], 4 * n2)
+        te.wait_ge(S["fw%d" % d], 2 * noff)
         te.wait_ge(S["ft%d" % d], 2 * noff)
         mm_tile(B, T["fw%dq" % d], T["fw%ds" % d], T["ft%dq" % d][:], T["ft%ds" % d][:], False, d == W_ROAD[-1])
     ve.wait_ge(S.lw3, 16)
     ve.quantize_mx(T.w3q[:], T.w3s[:], T.w3b[:]).then_inc(S.qw3, 1)
-    ve.wait_ge(S.pi0, noff)
-    ve.wait_ge(S.pi1, noff)
     for i in range(G):
         a = slice(NC * i, NC * i + NC)
+        for k in range(2):
+            for j, (b0, b1) in enumerate(P_PIECES[k]):
+                if b0 == i:
+                    ve.wait_ge(S["pi%d%d" % (k, j)], noff)
         ve.tensor_tensor(T.u[:, a], T.pi0[:, a], T.pi1[:, a], AluOpType.add).then_inc(S["u%d" % i], 1)
     for i in range(G):
         a, k = slice(NC * i, NC * i + NC), B + i
@@ -259,49 +269,44 @@ def rank_program(g, core, T, topo):
     g.wait_ge(S.qh, 1)
     for f, buf, sem in ((by, T.hq, S.rhc), (lambda v: v, T.hs, S.rhp)):
         g.remote_dma_fused([to(topo, helpers[0], near, sem, f(xcol(buf, r)), f(xcol(buf, r))),
-                            to(topo, T.cores[(r + H_FIRST) % N], off, S["h%d" % r], f(xcol(buf, r)), f(xcol(buf, r)))], local_sem=S.sh)
-    for d in H_NEXT:
-        send_slot("h", d, S.sh)
+                            to(topo, T.cores[(r + H_DIRECT[0]) % N], off, S["h%d" % r], f(xcol(buf, r)), f(xcol(buf, r)))], local_sem=S.sh)
+        sent["sh"] += noff + nnear
+    for d in H_DIRECT[1:]:
+        send_slot("h", d, "sh")
 
-    sy.wait_ge(S.sp0, noff)
-    sy.wait_ge(S.sp1, noff)
-    sy.wait_ge(S.stq, 2 * noff + 2 * count(near))
-    for c in range(N):
+    sy.wait_ge(S.sp0, sent["sp0"])
+    for i, c in enumerate((r, p1, q1, q2, p2)):
+        if i == 1:
+            sy.wait_ge(S.sp1, sent["sp1"])
         sy.wait_ge(S["qt%d" % c], 1)
         sy.dma_start(T.t[c], T.tb[:, TW * c:TW * c + TW]).then_inc(S.st, 16)
     stores = N
 
     te.wait_ge(S.qw3, 1)
     te.wait_ge(S.qh, 1)
-    for d in range(N):
+    for i, d in enumerate((0,) + H_DIRECT + H_HELPED):
         c = (r - d) % N
-        base = (A, B)[d % 2]
+        base = (A, B)[i % 2]
         if d:
             te.wait_ge(S["h%d" % c], 2 * noff)
         mm_tile(base, T.w3q, T.w3s, xcol(T.hq, c), xcol(T.hs, c))
         evac(base, lambda b: T.yb[:, TW * c + NC * b:TW * c + NC * b + NC], False)
-        if d < N - 1:
+        if i < N - 1:
             wait_ev(sy, base)
             sy.dma_start(T.y[:, TW * c:TW * c + TW], T.yb[:, TW * c:TW * c + TW]).then_inc(S.st, 16)
             stores += 1
-            if d == 0:
+            if i == 0:
                 sy.wait_ge(S.ha, G)
                 sy.dma_start(T.h[:], T.hb[:]).then_inc(S.st, 16)
                 stores += 1
         else:
             w = TW // 2
-            for k in (base, base + 1):
-                sy.wait_ge(S["ev%d" % k], ne[k])
+            wait_ev(sy, base, 0, 2)
             sy.dma_start(T.y[:, TW * c:TW * c + w], T.yb[:, TW * c:TW * c + w]).then_inc(S.st, 16)
             stores += 1
-            for k in (base + 2, base + 3):
-                ac.wait_ge(S["ev%d" % k], ne[k])
+            wait_ev(ac, base, 2, 4)
             ac.dma_start(T.y[:, TW * c + w:TW * c + TW], T.yb[:, TW * c + w:TW * c + TW]).then_inc(S.st2, 16)
     sy.wait_ge(S.st, 16 * stores)
     ac.wait_ge(S.st2, 16)
-    g.wait_ge(S.sx, 8 * noff)
-    g.wait_ge(S.sw, 2 * count(near))
-    g.wait_ge(S.sp0, noff)
-    g.wait_ge(S.sp1, noff)
-    g.wait_ge(S.stq, 2 * noff + 2 * count(near))
-    g.wait_ge(S.sh, 6 * noff + 2 * count(near))
+    for name in ("sx", "sw", "stq", "sp0", "sp1", "sh"):
+        g.wait_ge(S[name], sent[name])

import numpy as np
from concourse.bass import DstId, RemoteDMATransfer
from concourse.mybir import dt, AluOpType, ActivationFunctionType

N = 5
NC = 160
G = 4
TW = G * NC
SIM_CORES = 96
C1 = float(np.float32(0.047))
C2 = float(np.float32(0.02102))
W_ROAD = (1, 2)
T_HELPER = (0, 1)
P_ROAD = (3, 4)
P_PIECES = (((0, 1), (1, 4)), ((0, 1), (1, 3), (3, 4)))
X_ORDER = (3, 1, 4, 2)
H_DIRECT = (1, 2)
H_HELPED = (3, 4)

FP8 = "float8_e4m3fn_x4"
SCRATCH = {
    "xb": ("sbuf", [128, TW], "bfloat16"),
    "w1b": ("sbuf", [128, G * 512], "bfloat16"),
    "w2b": ("sbuf", [128, G * 512], "bfloat16"),
    "w3b": ("sbuf", [128, G * 512], "bfloat16"),
    "w1q": ("sbuf", [128, 512], FP8), "w1s": ("sbuf", [128, 512], "uint8"),
    "w2q": ("sbuf", [128, 512], FP8), "w2s": ("sbuf", [128, 512], "uint8"),
    "w3q": ("sbuf", [128, 512], FP8), "w3s": ("sbuf", [128, 512], "uint8"),
    "xq": ("sbuf", [128, N * NC], FP8), "xs": ("sbuf", [128, N * NC], "uint8"),
    "tb": ("sbuf", [128, N * TW], "bfloat16"),
    "tq": ("sbuf", [128, N * NC], FP8), "ts": ("sbuf", [128, N * NC], "uint8"),
    "fw1q": ("sbuf", [128, 512], FP8), "fw1s": ("sbuf", [128, 512], "uint8"),
    "fw2q": ("sbuf", [128, 512], FP8), "fw2s": ("sbuf", [128, 512], "uint8"),
    "ft1q": ("sbuf", [128, NC], FP8), "ft1s": ("sbuf", [128, NC], "uint8"),
    "ft2q": ("sbuf", [128, NC], FP8), "ft2s": ("sbuf", [128, NC], "uint8"),
    "po0": ("sbuf", [128, TW], "float32"), "po1": ("sbuf", [128, TW], "float32"),
    "pi0": ("sbuf", [128, TW], "float32"), "pi1": ("sbuf", [128, TW], "float32"),
    "u": ("sbuf", [128, TW], "float32"), "v": ("sbuf", [128, TW], "float32"),
    "hb": ("sbuf", [128, TW], "bfloat16"),
    "hq": ("sbuf", [128, N * NC], FP8), "hs": ("sbuf", [128, N * NC], "uint8"),
    "yb": ("sbuf", [128, N * TW], "float32"),
    "rwq": ("sbuf", [128, 256], FP8), "rws": ("sbuf", [128, 256], "uint8"),
    "rtq": ("sbuf", [128, NC], FP8), "rts": ("sbuf", [128, NC], "uint8"),
    "ps": ("psum", [128, 4096], "float32"),
}
SEMAPHORES = (["lx", "lw1", "lw3", "lw20", "lw21", "qw20", "qw21", "qx", "qw1", "qw3", "qh", "ha", "st", "st2",
               "sx", "sw", "stq", "sp0", "sp1", "sh", "rwc", "rwp", "rtc", "rtp", "rhc", "rhp", "s1", "s2", "s3",
               "fw1", "fw2", "ft1", "ft2"]
              + ["pi%d%d" % (k, j) for k in range(2) for j in range(len(P_PIECES[k]))]
              + ["pe%d" % b for b in range(8)] + ["ev%d" % b for b in range(8)] + ["u%d" % b for b in range(G)]
              + ["qt%d" % c for c in range(N)] + ["x%d" % c for c in range(N)] + ["h%d" % c for c in range(N)])


def bits(m):
    return [1 << b for b in range(m.bit_length()) if (m >> b) & 1]


def groups(m, n):
    e = bits(m)
    k = len(e) // n
    return [sum(e[i * k:(i + 1) * k]) for i in range(n)]


def count(m):
    return len(bits(m))


def to(topo, dst, mask, sem, dst_ap, src_ap):
    rid, pid, _ = topo.addr(dst)
    return RemoteDMATransfer(dst_ids=[DstId(rid=rid, pnc=pid)], dma_engine_mask=mask, remote_sem=sem, src=src_ap, dst=dst_ap)


def by(v):
    return v.bitcast(dt.uint8)


def xcol(buf, c):
    return buf[:, NC * c:NC * c + NC]


def helpers_of(topo, core):
    return [k for k in range(SIM_CORES) if topo.chip(k) == topo.chip(core) and topo.die(k) != topo.die(core)][:2]


def upper(topo, core, near, far):
    return topo.mask(core, near) & ~topo.mask(core, far)


def helper_program(g, core, T, topo, r, half):
    S = T.sem
    dests = [T.cores[(r + d) % N] for d in W_ROAD]
    off = topo.mask(core, dests[0])
    off2 = groups(off, 2)
    n_in, noff = count(upper(topo, T.cores[r], core, dests[0])), count(off)
    a, b = 256 * half, 256 * half + 256
    g.wait_ge(S.rwp, n_in)
    g.remote_dma_fused([to(topo, dests[k], off2[k], S["fw%d" % d], T["fw%ds" % d][:, a:b], T.rws[:, 0:256])
                        for k, d in enumerate(W_ROAD)], local_sem=S.s1)
    g.wait_ge(S.rwc, n_in)
    g.remote_dma_fused([to(topo, dests[k], off2[k], S["fw%d" % d], by(T["fw%dq" % d][:, a:b]), by(T.rwq[:, 0:256]))
                        for k, d in enumerate(W_ROAD)], local_sem=S.s1)
    d = W_ROAD[T_HELPER.index(half)]
    rid, pid, _ = topo.addr(T.cores[(r + d) % N])
    g.wait_ge(S.rtc, n_in)
    g.remote_dma(by(T["ft%dq" % d][:]), by(T.rtq[:]), S["ft%d" % d], S.s3, pid, rid, off)
    g.wait_ge(S.rtp, n_in)
    g.remote_dma(T["ft%ds" % d][:], T.rts[:], S["ft%d" % d], S.s3, pid, rid, off)
    if half == 0:
        for k, d in enumerate(H_HELPED):
            rid, pid, _ = topo.addr(T.cores[(r + d) % N])
            if k == 0:
                g.wait_ge(S.rhc, n_in)
            g.remote_dma(by(xcol(T.hq, r)), by(xcol(T.hq, r)), S["h%d" % r], S.s2, pid, rid, off)
            if k == 0:
                g.wait_ge(S.rhp, n_in)
            g.remote_dma(xcol(T.hs, r), xcol(T.hs, r), S["h%d" % r], S.s2, pid, rid, off)
        g.wait_ge(S.s2, 2 * len(H_HELPED) * noff)
    g.wait_ge(S.s3, 2 * noff)
    g.wait_ge(S.s1, 2 * noff)


def rank_program(g, core, T, topo):
    S = T.sem
    r = T.rank_of(core)
    if r is None:
        for k, c in enumerate(T.cores):
            hs = helpers_of(topo, c)
            if core in hs:
                helper_program(g, core, T, topo, k, hs.index(core))
        return
    helpers = helpers_of(topo, core)
    q1, q2, p1, p2 = [(r + d) % N for d in W_ROAD + P_ROAD]
    off = topo.mask(core, T.cores[q1])
    near = upper(topo, core, helpers[0], T.cores[q1])
    noff, nnear = count(off), count(near)
    te, ve, ac, sy = g.tensor, g.vector, g.scalar, g.sync
    RELU, COPY = ActivationFunctionType.Relu, ActivationFunctionType.Copy
    A, B = 0, 4
    nm, ne = [0] * 8, [0] * 8
    sent = {"sx": 0, "sw": 0, "stq": 0, "sp0": 0, "sp1": 0, "sh": 0}

    def bank(k):
        return T.ps[:, 512 * k:512 * k + NC]

    def mm_tile(base, wq, ws, xq, xs, start=True, stop=True):
        for b in range(G):
            k = base + b
            if start and ne[k]:
                te.wait_ge(S["ev%d" % k], ne[k])
            ins = te.matmul_mx(bank(k), wq[:, 128 * b:128 * b + 128], ws[:, 128 * b:128 * b + 128], xq, xs, start, stop)
            if stop:
                ins.then_inc(S["pe%d" % k], 1)
                nm[k] += 1

    def evac(base, out, relu):
        for b in range(G):
            k = base + b
            if b % 2 == 0:
                ac.wait_ge(S["pe%d" % k], nm[k])
                ins = ac.activation(out(b), bank(k), RELU, scale=C1) if relu else ac.activation(out(b), bank(k), COPY)
            else:
                ve.wait_ge(S["pe%d" % k], nm[k])
                ins = ve.tensor_scalar(out(b), bank(k), 0.0, C1, AluOpType.max, AluOpType.mult) if relu else ve.tensor_copy(out(b), bank(k))
            ins.then_inc(S["ev%d" % k], 1)
            ne[k] += 1

    def wait_ev(q, base, b0=0, b1=G):
        for k in range(base + b0, base + b1):
            q.wait_ge(S["ev%d" % k], ne[k])

    def first(base, c):
        if c != r:
            te.wait_ge(S["x%d" % c], 2 * noff)
        mm_tile(base, T.w1q, T.w1s, xcol(T.xq, c), xcol(T.xs, c))
        evac(base, lambda b: T.tb[:, TW * c + b:TW * c + TW:G], True)
        wait_ev(ve, base)
        ve.quantize_mx(xcol(T.tq, c), xcol(T.ts, c), T.tb[:, TW * c:TW * c + TW]).then_inc(S["qt%d" % c], 1)

    def send(dst, dst_ap, src_ap, sem, local, mask):
        rid, pid, _ = topo.addr(dst)
        g.remote_dma(dst_ap, src_ap, sem, S[local], pid, rid, mask)
        sent[local] += count(mask)

    def second(base, k, c):
        out = T["po%d" % k]
        te.wait_ge(S["qt%d" % c], 1)
        mm_tile(base, T.w2q, T.w2s, xcol(T.tq, c), xcol(T.ts, c))
        evac(base, lambda b: out[:, NC * b:NC * b + NC], False)
        for j, (b0, b1) in enumerate(P_PIECES[k]):
            wait_ev(g, base, b0, b1)
            w = slice(NC * b0, NC * b1)
            send(T.cores[c], T["pi%d" % k][:, w], out[:, w], S["pi%d%d" % (k, j)], "sp%d" % k, off)

    def send_slot(name, d, local, plane_first=False):
        q, s, sem = xcol(T[name + "q"], r), xcol(T[name + "s"], r), S["%s%d" % (name, r)]
        for v in ((s, by(q)) if plane_first else (by(q), s)):
            send(T.cores[(r + d) % N], v, v, sem, local, off)

    def send_w2(k):
        a = slice(256 * k, 256 * k + 256)
        g.wait_ge(S["qw2%d" % k], 1)
        send(helpers[k], T.rws[:, 0:256], T.w2s[:, a], S.rwp, "sw", near)
        send(helpers[k], by(T.rwq[:, 0:256]), by(T.w2q[:, a]), S.rwc, "sw", near)

    def send_t(k, c):
        g.wait_ge(S["qt%d" % c], 1)
        send(helpers[T_HELPER[k]], by(T.rtq[:]), by(xcol(T.tq, c)), S.rtc, "stq", near)
        send(helpers[T_HELPER[k]], T.rts[:], xcol(T.ts, c), S.rtp, "stq", near)

    sy.dma_start(T.xb[:], T.x[:]).then_inc(S.lx, 16)
    for k in range(2):
        sy.dma_start(T.w2b[:, 1024 * k:1024 * k + 1024], T.w2[:, 1024 * k:1024 * k + 1024]).then_inc(S["lw2%d" % k], 16)
    sy.dma_start(T.w1b[:], T.w1[:]).then_inc(S.lw1, 16)
    ve.wait_ge(S.lx, 16)
    ve.quantize_mx(xcol(T.xq, r), xcol(T.xs, r), T.xb[:]).then_inc(S.qx, 1)
    for k in range(2):
        a = slice(256 * k, 256 * k + 256)
        ve.wait_ge(S["lw2%d" % k], 16)
        ve.quantize_mx(T.w2q[:, a], T.w2s[:, a], T.w2b[:, 1024 * k:1024 * k + 1024]).then_inc(S["qw2%d" % k], 1)
    ve.wait_ge(S.lw1, 16)
    ve.quantize_mx(T.w1q[:], T.w1s[:], T.w1b[:]).then_inc(S.qw1, 1)
    g.wait_ge(S.qx, 1)
    for i, d in enumerate(X_ORDER):
        send_slot("x", N - d, "sx", i == 0)
        if i < 2:
            send_w2(i)
    sy.wait_ge(S["x%d" % p1], 2 * noff)
    sy.dma_start(T.w3b[:], T.w3[:]).then_inc(S.lw3, 16)

    te.wait_ge(S.qx, 1)
    te.wait_ge(S.qw1, 1)
    first(A, r)
    first(B, p1)
    first(A, q1)
    te.wait_ge(S.qw20, 1)
    te.wait_ge(S.qw21, 1)
    second(B, 0, p1)
    send_t(0, q1)
    first(A, p2)
    first(B, q2)
    send_t(1, q2)
    second(A, 1, p2)

    te.wait_ge(S["qt%d" % r], 1)
    mm_tile(B, T.w2q, T.w2s, xcol(T.tq, r), xcol(T.ts, r), True, False)
    for d in W_ROAD:
        te.wait_ge(S["fw%d" % d], 2 * noff)
        te.wait_ge(S["ft%d" % d], 2 * noff)
        mm_tile(B, T["fw%dq" % d], T["fw%ds" % d], T["ft%dq" % d][:], T["ft%ds" % d][:], False, d == W_ROAD[-1])
    ve.wait_ge(S.lw3, 16)
    ve.quantize_mx(T.w3q[:], T.w3s[:], T.w3b[:]).then_inc(S.qw3, 1)
    for i in range(G):
        a = slice(NC * i, NC * i + NC)
        for k in range(2):
            for j, (b0, b1) in enumerate(P_PIECES[k]):
                if b0 == i:
                    ve.wait_ge(S["pi%d%d" % (k, j)], noff)
        ve.tensor_tensor(T.u[:, a], T.pi0[:, a], T.pi1[:, a], AluOpType.add).then_inc(S["u%d" % i], 1)
    for i in range(G):
        a, k = slice(NC * i, NC * i + NC), B + i
        ve.wait_ge(S["u%d" % i], 1)
        ve.wait_ge(S["pe%d" % k], nm[k])
        ve.tensor_tensor(T.v[:, a], bank(k), T.u[:, a], AluOpType.add).then_inc(S["ev%d" % k], 1)
        ne[k] += 1
        ac.wait_ge(S["ev%d" % k], ne[k])
        ac.activation(T.hb[:, i:TW:G], T.v[:, a], RELU, scale=C2).then_inc(S.ha, 1)
    ve.wait_ge(S.ha, G)
    ve.quantize_mx(xcol(T.hq, r), xcol(T.hs, r), T.hb[:]).then_inc(S.qh, 1)
    g.wait_ge(S.qh, 1)
    for f, buf, sem in ((by, T.hq, S.rhc), (lambda v: v, T.hs, S.rhp)):
        g.remote_dma_fused([to(topo, helpers[0], near, sem, f(xcol(buf, r)), f(xcol(buf, r))),
                            to(topo, T.cores[(r + H_DIRECT[0]) % N], off, S["h%d" % r], f(xcol(buf, r)), f(xcol(buf, r)))], local_sem=S.sh)
        sent["sh"] += noff + nnear
    for d in H_DIRECT[1:]:
        send_slot("h", d, "sh")

    sy.wait_ge(S.sp0, sent["sp0"])
    for i, c in enumerate((r, p1, q1, q2, p2)):
        if i == 1:
            sy.wait_ge(S.sp1, sent["sp1"])
        sy.wait_ge(S["qt%d" % c], 1)
        sy.dma_start(T.t[c], T.tb[:, TW * c:TW * c + TW]).then_inc(S.st, 16)
    stores = N

    te.wait_ge(S.qw3, 1)
    te.wait_ge(S.qh, 1)
    for i, d in enumerate((0,) + H_DIRECT + H_HELPED):
        c = (r - d) % N
        base = (A, B)[i % 2]
        if d:
            te.wait_ge(S["h%d" % c], 2 * noff)
        mm_tile(base, T.w3q, T.w3s, xcol(T.hq, c), xcol(T.hs, c))
        evac(base, lambda b: T.yb[:, TW * c + NC * b:TW * c + NC * b + NC], False)
        if i < N - 1:
            wait_ev(sy, base)
            sy.dma_start(T.y[:, TW * c:TW * c + TW], T.yb[:, TW * c:TW * c + TW]).then_inc(S.st, 16)
            stores += 1
            if i == 0:
                sy.wait_ge(S.ha, G)
                sy.dma_start(T.h[:], T.hb[:]).then_inc(S.st, 16)
                stores += 1
        else:
            w = TW // 2
            wait_ev(sy, base, 0, 2)
            sy.dma_start(T.y[:, TW * c:TW * c + w], T.yb[:, TW * c:TW * c + w]).then_inc(S.st, 16)
            stores += 1
            wait_ev(ac, base, 2, 4)
            ac.dma_start(T.y[:, TW * c + w:TW * c + TW], T.yb[:, TW * c + w:TW * c + TW]).then_inc(S.st2, 16)
    sy.wait_ge(S.st, 16 * stores)
    ac.wait_ge(S.st2, 16)
    for name in ("sx", "sw", "stq", "sp0", "sp1", "sh"):
        g.wait_ge(S[name], sent[name])
